import numpy as np
import ml_dtypes


def mxq(x, axis, fmt="e4m3"):
    dtype, down = {"e4m3": (ml_dtypes.float8_e4m3fn, 7), "e5m2": (ml_dtypes.float8_e5m2, 14)}[fmt]
    v = np.moveaxis(np.asarray(x, np.float32).astype(ml_dtypes.bfloat16).astype(np.float64), axis, -1)
    blocks = v.reshape(v.shape[:-1] + (-1, 32))
    amax = np.abs(blocks).max(-1, keepdims=True)
    byte = np.maximum(np.where(amax > 0, np.frexp(amax)[1] - 1 + 127, 0) - down, 1)
    scale = np.exp2(byte - 127.0)
    codes = (blocks / scale).astype(np.float32).astype(dtype).astype(np.float64)
    return np.moveaxis((codes * scale).reshape(v.shape), -1, axis)


WIDE = False


def mx_kscale(k):
    if not WIDE:
        return np.ones(k)
    levels = np.array([10, -10, 5, -5, 0])
    if k % 512:
        return np.exp2(np.random.permutation(np.resize(levels, k // 32))).repeat(32)
    a = np.empty((k // 512, 16))
    for p in range(k // 512):
        a[p, :8] = np.random.permutation(np.resize(levels, 8))
        for g in range(8):
            far = levels[np.abs(levels - a[p, g]) >= 10]
            a[p, g + 8] = far[np.random.randint(len(far))]
    return np.exp2(a.ravel()).repeat(32)


def f64(x):
    return np.asarray(x).astype(np.float64)


def striped(idx):
    return np.tile(idx.reshape(-1, 16).T, (8, 1)).astype(np.uint16)


def unstriped(offs):
    return offs[:16].T.reshape(-1).astype(np.int64)


def pack_weight(w):
    k, n = w.shape
    w = f64(np.asarray(w, np.float32).astype(ml_dtypes.bfloat16)).reshape(k // 32, 32, n)
    amax = np.abs(w).max(1)
    byte = np.clip(np.where(amax > 0, np.frexp(amax)[1] - 1 + 127 - 7, 1), 1, 254)
    scaled = (w * np.exp2(127.0 - byte)[:, None, :]).reshape(k, n).astype(np.float32)
    words = np.ascontiguousarray(scaled.reshape(k // 512, 128, 4, n).transpose(0, 1, 3, 2)).astype(ml_dtypes.float8_e4m3fn).view(np.uint8)
    return words, np.ascontiguousarray(byte.astype(np.uint8).reshape(k // 512, 16, n))


def unpack_weight(words, scales):
    g, p, n, _ = words.shape
    vals = np.ascontiguousarray(words).view(ml_dtypes.float8_e4m3fn).astype(np.float64) * np.repeat(np.exp2(scales.astype(np.float64) - 127.0), 8, axis=1)[..., None]
    return vals.transpose(0, 1, 3, 2).reshape(g * 512, n)


def gelu(v):
    return 0.5 * v * (1.0 + np.tanh(np.sqrt(2.0 / np.pi) * (v + 0.044715 * v**3)))


K, T, E, C, N = 2048, 1024, 12, 128, 128
TOP = 3
PAD = 64


def by_expert(wq, xq):
    return np.concatenate([wq[e].T @ xq[:, e * C:(e + 1) * C] for e in range(E)], axis=1)


def setup_inputs():
    n = np.random.standard_normal
    s = mx_kscale(K)[:, None]
    slot_token = np.empty(E * C, np.int64); pos = np.tile(E * C + np.arange(T) % PAD, (TOP, 1)); taken = np.zeros(T, np.int64)
    liked = np.random.randn(T)
    for e in np.random.permutation(E):
        free = np.flatnonzero(taken < TOP); pick = np.random.permutation(free[np.argsort(-(liked[free] + np.random.gumbel(size=free.size)))[:C]]); slot_token[e * C:(e + 1) * C] = pick
        pos[taken[pick], pick] = e * C + np.arange(C); taken[pick] += 1
    g = np.random.uniform(0.2, 0.8, (TOP, T))
    packed = [pack_weight(m) for m in n((E, K, N)) / np.sqrt(K) / s[None]]
    return {
        "xT": (n((K, T)) * s).astype(np.float32),
        "w_words": np.stack([m[0] for m in packed]),
        "w_scales": np.stack([m[1] for m in packed]),
        "b": (0.3 * n((N, E))).astype(np.float32),
        "gate": np.stack([np.tile(r, (N, 1)) for r in g]).astype(np.float32),
        "offs": striped(slot_token),
        "pos1": striped(pos[0]),
        "pos2": striped(pos[1]),
        "pos3": striped(pos[2]),
    }


def reference(xT, w_words, w_scales, b, gate, offs, pos1, pos2, pos3):
    idx = unstriped(offs)
    w = np.stack([unpack_weight(w_words[e], w_scales[e]) for e in range(E)])
    xq = mxq(f64(xT)[:, idx], 0, "e4m3")
    y = by_expert(w, xq)
    y = gelu(y + np.repeat(f64(b), C, axis=1))
    y = np.concatenate([y, np.zeros((N, PAD))], axis=1)
    return sum(f64(gate[r]) * y[:, unstriped(p)] for r, p in enumerate((pos1, pos2, pos3)))

@@ -1,0 +1,185 @@
+from contextlib import ExitStack
+
+import concourse.mybir as mybir
+from concourse.masks import make_identity
+
+K, T, E, C, N = 2048, 1024, 12, 128, 128
+TOP, PAD = 3, 64
+S = E * C
+P = 128
+PACK = 4
+K_PASS = P * PACK
+PASSES = K // K_PASS
+PER_COL = 16
+
+F32 = mybir.dt.float32
+BF16 = mybir.dt.bfloat16
+I32 = mybir.dt.int32
+U32 = mybir.dt.uint32
+U16 = mybir.dt.uint16
+U8 = mybir.dt.uint8
+FP8X4 = mybir.dt.float8_e4m3fn_x4
+COPY = mybir.ActivationFunctionType.Copy
+GELU = mybir.ActivationFunctionType.Gelu_apprx_tanh
+MULT = mybir.AluOpType.mult
+ADD = mybir.AluOpType.add
+
+FLOPS = 2 * K * N * S
+BYTES = 4 * K * T + E * K * N + E * K * N // 32 + 4 * N * E + 4 * TOP * T + 2 * P * (S + TOP * T) // PER_COL + 4 * N * T
+
+X_LOADS = ((1024,), (1024,), (1024,), (1024,))
+X_PIECES = ((512, 256, 256), (512, 256, 256), (512, 256, 256), (512, 256, 256))
+VECTOR_TOKENS = ((0, 0),)
+W_GROUPS = (3, 3, 3, 2, 1)
+HALF = S // 2
+LAST_WORD_CUTS = (768, 512, 256)
+OUT_CUTS = (512, 256, 256)
+
+
+def runs(widths):
+    ends = [sum(widths[: i + 1]) for i in range(len(widths))]
+    return [(end - width, end) for width, end in zip(widths, ends)]
+
+
+def tile_moe_ecr_lin_gelu_kernel(
+    tc, xT, w_words, w_scales, b, gate, offs, pos1, pos2, pos3, out
+):
+    nc = tc.nc
+    with ExitStack() as ctx:
+        keep = ctx.enter_context(tc.tile_pool(name="keep", bufs=1))
+        psum = ctx.enter_context(tc.psum_pool(name="psum", bufs=8))
+
+        def load_list(name, src):
+            tile = keep.tile(list(src.shape), U16, name=name)
+            nc.sync.dma_start(tile[:], src)
+            return tile
+
+        def load_x(a, t0, t1):
+            raw = keep.tile([P, PACK, t1 - t0], F32, name=f"raw{a}_{t0}")
+            rows = xT[a * K_PASS : (a + 1) * K_PASS, t0:t1]
+            nc.sync.dma_start(raw[:], rows.rearrange("(p j) w -> p j w", j=PACK))
+            return raw
+
+        w_planes = keep.tile([P, E * PASSES, N], U8, align_bytes=64)
+        nc.vector.memset(w_planes[:].bitcast(I32), 0)
+        x_planes = keep.tile([P, T], U8, align_bytes=64)
+        nc.vector.memset(x_planes[:].bitcast(I32), 0)
+        zeros = keep.tile([P, PAD], F32)
+        nc.vector.memset(zeros[:], 0.0)
+        y = keep.tile([P, S + PAD], F32)
+        nc.scalar.activation(y[:, S:], zeros[:], GELU)
+        ident = keep.tile([P, P], F32)
+        make_identity(nc, ident[:])
+
+        gate_cols = keep.tile([P, TOP, T // P], F32)
+        raws = {}
+        lists = {}
+        bias = keep.tile([P, E], F32)
+        for a in range(PASSES):
+            for t0, t1 in runs(X_LOADS[a]):
+                raw = load_x(a, t0, t1)
+                for c0, c1 in runs(X_PIECES[a]):
+                    if t0 <= c0 < t1:
+                        raws[a, c0] = raw[:, :, c0 - t0 : c1 - t0]
+            if a == 0:
+                slots = load_list("slots", offs)
+            if a == 1:
+                nc.sync.dma_start(bias[:], b)
+                lists[0] = load_list("pos1", pos1)
+            if a == 2:
+                lists[1] = load_list("pos2", pos2)
+                lists[2] = load_list("pos3", pos3)
+        nc.sync.dma_start(gate_cols[:], gate[:, 0, :].rearrange("r (p i) -> p r i", p=P))
+        scale_rows = w_scales.rearrange("e a (quad q) n -> q quad (e a) n", q=4).bitcast(I32)
+        for q in range(4):
+            nc.gpsimd.dma_start(w_planes[:].bitcast(I32)[q:P:32], scale_rows[q])
+        w_codes = {}
+        w_view = w_words.rearrange("e a p n r -> p (e a) (n r)").bitcast(I32)
+        for e0, e1 in runs(W_GROUPS):
+            words = keep.tile([P, (e1 - e0) * PASSES, N], I32, name=f"w{e0}", align_bytes=64)
+            nc.sync.dma_start(words[:], w_view[:, e0 * PASSES : e1 * PASSES, :])
+            for e in range(e0, e1):
+                for a in range(PASSES):
+                    w_codes[e, a] = words[:, (e - e0) * PASSES + a, :]
+
+        def gather(dst, window, s0, s1):
+            nc.vector.tensor_copy(dst[:, s0:s1], window[:].indirect(slots[:, s0 // PER_COL : s1 // PER_COL]))
+
+        slot_codes = []
+        slot_planes = keep.tile([P, S], U8, align_bytes=64)
+        for a in range(PASSES):
+            codes = keep.tile([P, T], U32, name=f"codes{a}", align_bytes=64)
+            for t0, t1 in runs(X_PIECES[a]):
+                raw = raws[a, t0]
+                grouped = keep.tile([P, t1 - t0, PACK], BF16, name=f"grouped{a}_{t0}", align_bytes=64)
+                dst = grouped[:].rearrange("p (c i) j -> p c j i", i=4)
+                src = raw.rearrange("p j (c i) -> p c j i", i=4)
+                if (a, t0) in VECTOR_TOKENS:
+                    nc.vector.tensor_copy(dst, src)
+                else:
+                    nc.scalar.activation(dst, src, COPY)
+                nc.vector.quantize_mx(
+                    codes[:, t0:t1].bitcast(FP8X4),
+                    x_planes[4 * a : P, t0:t1],
+                    grouped[:].rearrange("p w j -> p (w j)"),
+                )
+            picked = keep.tile([P, S], U32, name=f"picked{a}", align_bytes=64)
+            slot_codes.append(picked)
+            if a < PASSES - 1:
+                for s0, s1 in runs((HALF, HALF)):
+                    gather(picked, codes, s0, s1)
+            else:
+                for s0, s1 in runs(LAST_WORD_CUTS):
+                    if s0 % HALF == 0:
+                        gather(slot_planes, x_planes, s0, s0 + HALF)
+                    gather(picked, codes, s0, s1)
+
+        gates = []
+        for r in range(TOP):
+            spread = keep.tile([P, T], F32, name=f"gate{r}")
+            for h in range(2):
+                bank = psum.tile([P, 4 * P], F32, name="bank")
+                for i in range(4):
+                    column = gate_cols[:, r, 4 * h + i : 4 * h + i + 1]
+                    nc.tensor.transpose(bank[:, i * P : (i + 1) * P], column.to_broadcast([P, P]), ident[:])
+                nc.scalar.copy(
+                    spread[:].rearrange("n (p h i) -> n h p i", h=2, i=4)[:, h],
+                    bank[:].rearrange("n (i p) -> n p i", i=4),
+                )
+            gates.append(spread)
+
+        for e in range(E):
+            cols = slice(e * C, (e + 1) * C)
+            acc = psum.tile([P, C], F32, name="bank")
+            for a in range(PASSES):
+                nc.tensor.matmul_mx(
+                    acc[:],
+                    lhsT=w_codes[e, a].bitcast(FP8X4),
+                    lhsT_scale=w_planes[:, e * PASSES + a, :],
+                    rhs=slot_codes[a][:, cols].bitcast(FP8X4),
+                    rhs_scale=slot_planes[4 * a : P, cols],
+                    start=(a == 0),
+                    stop=(a == PASSES - 1),
+                )
+            nc.scalar.activation(y[:, cols], acc[:], GELU, bias=bias[:, e : e + 1])
+
+        pending = None
+        for t0, t1 in runs(OUT_CUTS):
+            terms = []
+            for r in range(TOP):
+                term = keep.tile([P, t1 - t0], F32, name=f"term{r}_{t0}")
+                picks = lists[r][:, t0 // PER_COL : t1 // PER_COL]
+                nc.vector.tensor_tensor(term[:], y[:].indirect(picks), gates[r][:, t0:t1], MULT)
+                terms.append(term)
+                if r == 0 and pending is not None:
+                    pending()
+            pair = keep.tile([P, t1 - t0], F32, name=f"pair{t0}")
+            nc.vector.tensor_tensor(pair[:], terms[0][:], terms[1][:], ADD)
+
+            def finish(pair=pair, last=terms[2], t0=t0, t1=t1):
+                total = keep.tile([P, t1 - t0], F32, name=f"total{t0}")
+                nc.vector.tensor_tensor(total[:], pair[:], last[:], ADD)
+                nc.sync.dma_start(out[:, t0:t1], total[:])
+
+            pending = finish
+        pending()

@@ -73,7 +73,6 @@ def tile_moe_ecr_lin_gelu_kernel(
 
         gate_cols = keep.tile([P, TOP, T // P], F32)
         raws = {}
-        lists = {}
         bias = keep.tile([P, E], F32)
         for a in range(PASSES):
             for t0, t1 in runs(X_LOADS[a]):
@@ -85,14 +84,10 @@ def tile_moe_ecr_lin_gelu_kernel(
                 slots = load_list("slots", offs)
             if a == 1:
                 nc.sync.dma_start(bias[:], b)
-                lists[0] = load_list("pos1", pos1)
-            if a == 2:
-                lists[1] = load_list("pos2", pos2)
-                lists[2] = load_list("pos3", pos3)
         nc.sync.dma_start(gate_cols[:], gate[:, 0, :].rearrange("r (p i) -> p r i", p=P))
         scale_rows = w_scales.rearrange("e a (quad q) n -> q quad (e a) n", q=4).bitcast(I32)
         for q in range(4):
-            nc.gpsimd.dma_start(w_planes[:].bitcast(I32)[q:P:32], scale_rows[q])
+            nc.sync.dma_start(w_planes[:].bitcast(I32)[q:P:32], scale_rows[q])
         w_codes = {}
         w_view = w_words.rearrange("e a p n r -> p (e a) (n r)").bitcast(I32)
         for e0, e1 in runs(W_GROUPS):
@@ -101,6 +96,8 @@ def tile_moe_ecr_lin_gelu_kernel(
             for e in range(e0, e1):
                 for a in range(PASSES):
                     w_codes[e, a] = words[:, (e - e0) * PASSES + a, :]
+
+        lists = [load_list(f"pos{r + 1}", src) for r, src in enumerate((pos1, pos2, pos3))]
 
         def gather(dst, window, s0, s1):
             nc.vector.tensor_copy(dst[:, s0:s1], window[:].indirect(slots[:, s0 // PER_COL : s1 // PER_COL]))
@@ -148,12 +145,14 @@ def tile_moe_ecr_lin_gelu_kernel(
                 )
             gates.append(spread)
 
-        for e in range(E):
-            cols = slice(e * C, (e + 1) * C)
-            acc = psum.tile([P, C], F32, name="bank")
-            for a in range(PASSES):
+        for e0, e1 in runs(LAST_WORD_CUTS):
+            group = range(e0 // C, e1 // C)
+            accs = {e: psum.tile([P, C], F32, name="bank") for e in group}
+            steps = [(e, a) for e in group for a in range(PASSES - 1)] + [(e, PASSES - 1) for e in group]
+            for e, a in steps:
+                cols = slice(e * C, (e + 1) * C)
                 nc.tensor.matmul_mx(
-                    acc[:],
+                    accs[e][:],
                     lhsT=w_codes[e, a].bitcast(FP8X4),
                     lhsT_scale=w_planes[:, e * PASSES + a, :],
                     rhs=slot_codes[a][:, cols].bitcast(FP8X4),
@@ -161,7 +160,8 @@ def tile_moe_ecr_lin_gelu_kernel(
                     start=(a == 0),
                     stop=(a == PASSES - 1),
                 )
-            nc.scalar.activation(y[:, cols], acc[:], GELU, bias=bias[:, e : e + 1])
+                if a == PASSES - 1:
+                    nc.scalar.activation(y[:, cols], accs[e][:], GELU, bias=bias[:, e : e + 1])
 
         pending = None
         for t0, t1 in runs(OUT_CUTS):

@@ -27,9 +27,9 @@ ADD = mybir.AluOpType.add
 FLOPS = 2 * K * N * S
 BYTES = 4 * K * T + E * K * N + E * K * N // 32 + 4 * N * E + 4 * TOP * T + 2 * P * (S + TOP * T) // PER_COL + 4 * N * T
 
-X_LOADS = ((1024,), (1024,), (1024,), (1024,))
-X_PIECES = ((512, 256, 256), (512, 256, 256), (512, 256, 256), (512, 256, 256))
-VECTOR_TOKENS = ((0, 0),)
+X_LOADS = ((256, 256, 256, 128, 128), (256, 256, 256, 256), (256, 256, 256, 256), (512, 256, 256))
+X_PIECES = X_LOADS
+VECTOR_TOKENS = ((0, 0), (0, 256), (0, 512), (0, 768))
 W_GROUPS = (3, 3, 3, 2, 1)
 HALF = S // 2
 LAST_WORD_CUTS = (768, 512, 256)
@@ -100,12 +100,15 @@ def tile_moe_ecr_lin_gelu_kernel(
         lists = [load_list(f"pos{r + 1}", src) for r, src in enumerate((pos1, pos2, pos3))]
 
         def gather(dst, window, s0, s1):
-            nc.vector.tensor_copy(dst[:, s0:s1], window[:].indirect(slots[:, s0 // PER_COL : s1 // PER_COL]))
+            nc.vector.tensor_copy(dst[:, s0:s1], window.indirect(slots[:, s0 // PER_COL : s1 // PER_COL]))
 
         slot_codes = []
+        all_codes = keep.tile([P, (PASSES + 1) * T], U32, align_bytes=64)
+        nc.vector.memset(all_codes[:, PASSES * T :], 0)
         slot_planes = keep.tile([P, S], U8, align_bytes=64)
         for a in range(PASSES):
-            codes = keep.tile([P, T], U32, name=f"codes{a}", align_bytes=64)
+            first = (PASSES - 1 - a) * T
+            codes = all_codes[:, first : first + T]
             for t0, t1 in runs(X_PIECES[a]):
                 raw = raws[a, t0]
                 grouped = keep.tile([P, t1 - t0, PACK], BF16, name=f"grouped{a}_{t0}", align_bytes=64)
@@ -123,12 +126,11 @@ def tile_moe_ecr_lin_gelu_kernel(
             picked = keep.tile([P, S], U32, name=f"picked{a}", align_bytes=64)
             slot_codes.append(picked)
             if a < PASSES - 1:
-                for s0, s1 in runs((HALF, HALF)):
-                    gather(picked, codes, s0, s1)
+                gather(picked, all_codes[:, first : first + 2 * T], 0, S)
             else:
                 for s0, s1 in runs(LAST_WORD_CUTS):
                     if s0 % HALF == 0:
-                        gather(slot_planes, x_planes, s0, s0 + HALF)
+                        gather(slot_planes, x_planes[:], s0, s0 + HALF)
                     gather(picked, codes, s0, s1)
 
         gates = []
@@ -163,23 +165,30 @@ def tile_moe_ecr_lin_gelu_kernel(
                 if a == PASSES - 1:
                     nc.scalar.activation(y[:, cols], accs[e][:], GELU, bias=bias[:, e : e + 1])
 
-        pending = None
-        for t0, t1 in runs(OUT_CUTS):
+        chunks = runs(OUT_CUTS)
+        for t0, t1 in chunks:
+            width = t1 - t0
+            blocks = runs((P,) * (width // P))
+            on_tensor = t1 < T
             terms = []
+            turned = [psum.tile([P, P], F32, name="bank") for block in blocks] if on_tensor else []
             for r in range(TOP):
-                term = keep.tile([P, t1 - t0], F32, name=f"term{r}_{t0}")
+                term = keep.tile([P, width], F32, name=f"term{r}_{t0}")
                 picks = lists[r][:, t0 // PER_COL : t1 // PER_COL]
                 nc.vector.tensor_tensor(term[:], y[:].indirect(picks), gates[r][:, t0:t1], MULT)
                 terms.append(term)
-                if r == 0 and pending is not None:
-                    pending()
-            pair = keep.tile([P, t1 - t0], F32, name=f"pair{t0}")
-            nc.vector.tensor_tensor(pair[:], terms[0][:], terms[1][:], ADD)
-
-            def finish(pair=pair, last=terms[2], t0=t0, t1=t1):
-                total = keep.tile([P, t1 - t0], F32, name=f"total{t0}")
-                nc.vector.tensor_tensor(total[:], pair[:], last[:], ADD)
-                nc.sync.dma_start(out[:, t0:t1], total[:])
-
-            pending = finish
-        pending()
+                for bank, (c0, c1) in zip(turned, blocks):
+                    nc.tensor.matmul(bank[:], term[:, c0:c1], ident[:], start=(r == 0), stop=(r == TOP - 1), is_transpose=True)
+            total = keep.tile([P, width], F32, name=f"total{t0}")
+            if on_tensor:
+                by_token = keep.tile([P, width], F32, name=f"by_token{t0}")
+                back = psum.tile([P, width], F32, name="bank")
+                for bank, (c0, c1) in zip(turned, blocks):
+                    nc.scalar.copy(by_token[:, c0:c1], bank[:])
+                    nc.tensor.transpose(back[:, c0:c1], by_token[:, c0:c1], ident[:])
+                nc.scalar.copy(total[:], back[:])
+            else:
+                pair = keep.tile([P, width], F32)
+                nc.vector.tensor_tensor(pair[:], terms[0][:], terms[1][:], ADD)
+                nc.vector.tensor_tensor(total[:], pair[:], terms[2][:], ADD)
+            nc.sync.dma_start(out[:, t0:t1], total[:])

@@ -27,10 +27,10 @@ ADD = mybir.AluOpType.add
 FLOPS = 2 * K * N * S
 BYTES = 4 * K * T + E * K * N + E * K * N // 32 + 4 * N * E + 4 * TOP * T + 2 * P * (S + TOP * T) // PER_COL + 4 * N * T
 
-X_LOADS = ((256, 256, 256, 128, 128), (256, 256, 256, 256), (256, 256, 256, 256), (512, 256, 256))
-X_PIECES = X_LOADS
-VECTOR_TOKENS = ((0, 0), (0, 256), (0, 512), (0, 768))
-W_GROUPS = (3, 3, 3, 2, 1)
+X_LOADS = ((1024,), (1024,), (1024,), (1024,))
+X_PIECES = ((512, 256, 256), (512, 256, 256), (512, 256, 256), (512, 256, 256))
+VECTOR_TOKENS = ((0, 0),)
+W_GROUPS = (12, 12, 8, 8, 4, 2, 2)
 HALF = S // 2
 LAST_WORD_CUTS = (768, 512, 256)
 OUT_CUTS = (512, 256, 256)
@@ -90,12 +90,11 @@ def tile_moe_ecr_lin_gelu_kernel(
             nc.sync.dma_start(w_planes[:].bitcast(I32)[q:P:32], scale_rows[q])
         w_codes = {}
         w_view = w_words.rearrange("e a p n r -> p (e a) (n r)").bitcast(I32)
-        for e0, e1 in runs(W_GROUPS):
-            words = keep.tile([P, (e1 - e0) * PASSES, N], I32, name=f"w{e0}", align_bytes=64)
-            nc.sync.dma_start(words[:], w_view[:, e0 * PASSES : e1 * PASSES, :])
-            for e in range(e0, e1):
-                for a in range(PASSES):
-                    w_codes[e, a] = words[:, (e - e0) * PASSES + a, :]
+        for m0, m1 in runs(W_GROUPS):
+            words = keep.tile([P, m1 - m0, N], I32, name=f"w{m0}", align_bytes=64)
+            nc.sync.dma_start(words[:], w_view[:, m0:m1, :])
+            for m in range(m0, m1):
+                w_codes[divmod(m, PASSES)] = words[:, m - m0, :]
 
         lists = [load_list(f"pos{r + 1}", src) for r, src in enumerate((pos1, pos2, pos3))]
 
@@ -147,8 +146,8 @@ def tile_moe_ecr_lin_gelu_kernel(
                 )
             gates.append(spread)
 
-        for e0, e1 in runs(LAST_WORD_CUTS):
-            group = range(e0 // C, e1 // C)
+        for e0, e1 in runs((E // 2,) + (1,) * (E // 2)):
+            group = range(e0, e1)
             accs = {e: psum.tile([P, C], F32, name="bank") for e in group}
             steps = [(e, a) for e in group for a in range(PASSES - 1)] + [(e, PASSES - 1) for e in group]
             for e, a in steps:

@@ -4,13 +4,20 @@ import concourse.mybir as mybir
 from concourse.masks import make_identity
 
 K, T, E, C, N = 2048, 1024, 12, 128, 128
-TOP, PAD = 3, 64
+TOP = 3
+PAD = 64
 S = E * C
 P = 128
 PACK = 4
 K_PASS = P * PACK
 PASSES = K // K_PASS
+LAST = PASSES - 1
 PER_COL = 16
+QUAD = 32
+QUAD_ROWS = 4
+LINE = 4
+BANKS = 8
+BANK_BLOCKS = 4
 
 F32 = mybir.dt.float32
 BF16 = mybir.dt.bfloat16
@@ -27,13 +34,12 @@ ADD = mybir.AluOpType.add
 FLOPS = 2 * K * N * S
 BYTES = 4 * K * T + E * K * N + E * K * N // 32 + 4 * N * E + 4 * TOP * T + 2 * P * (S + TOP * T) // PER_COL + 4 * N * T
 
-X_LOADS = ((1024,), (1024,), (1024,), (1024,))
-X_PIECES = ((512, 256, 256), (512, 256, 256), (512, 256, 256), (512, 256, 256))
-VECTOR_TOKENS = ((0, 0),)
-W_GROUPS = (12, 12, 8, 8, 4, 2, 2)
-HALF = S // 2
-LAST_WORD_CUTS = (768, 512, 256)
-OUT_CUTS = (512, 256, 256)
+X_PIECES = ((512, 256, 256), (512, 256, 256), (512, 256, 128, 128), (512, 256, 256))
+VECTOR_PIECES = ((0, 0), (1, 768), (2, 896))
+W_LOADS = (12, 12, 8, 8, 4, 3, 1)
+SLOT_GROUPS = (768, 384, 256, 128)
+BYTE_SLOTS = S // 2
+OUT_STRETCHES = (512, 256, 256)
 
 
 def runs(widths):
@@ -47,23 +53,17 @@ def tile_moe_ecr_lin_gelu_kernel(
     nc = tc.nc
     with ExitStack() as ctx:
         keep = ctx.enter_context(tc.tile_pool(name="keep", bufs=1))
-        psum = ctx.enter_context(tc.psum_pool(name="psum", bufs=8))
+        psum = ctx.enter_context(tc.psum_pool(name="psum", bufs=BANKS))
 
         def load_list(name, src):
             tile = keep.tile(list(src.shape), U16, name=name)
             nc.sync.dma_start(tile[:], src)
             return tile
 
-        def load_x(a, t0, t1):
-            raw = keep.tile([P, PACK, t1 - t0], F32, name=f"raw{a}_{t0}")
-            rows = xT[a * K_PASS : (a + 1) * K_PASS, t0:t1]
-            nc.sync.dma_start(raw[:], rows.rearrange("(p j) w -> p j w", j=PACK))
-            return raw
-
         w_planes = keep.tile([P, E * PASSES, N], U8, align_bytes=64)
         nc.vector.memset(w_planes[:].bitcast(I32), 0)
-        x_planes = keep.tile([P, T], U8, align_bytes=64)
-        nc.vector.memset(x_planes[:].bitcast(I32), 0)
+        x_plane = keep.tile([P, T], U8, align_bytes=64)
+        nc.vector.memset(x_plane[:].bitcast(I32), 0)
         zeros = keep.tile([P, PAD], F32)
         nc.vector.memset(zeros[:], 0.0)
         y = keep.tile([P, S + PAD], F32)
@@ -72,100 +72,96 @@ def tile_moe_ecr_lin_gelu_kernel(
         make_identity(nc, ident[:])
 
         gate_cols = keep.tile([P, TOP, T // P], F32)
-        raws = {}
         bias = keep.tile([P, E], F32)
+        x_rows = []
         for a in range(PASSES):
-            for t0, t1 in runs(X_LOADS[a]):
-                raw = load_x(a, t0, t1)
-                for c0, c1 in runs(X_PIECES[a]):
-                    if t0 <= c0 < t1:
-                        raws[a, c0] = raw[:, :, c0 - t0 : c1 - t0]
+            rows = keep.tile([P, PACK, T], F32, name=f"x_rows{a}")
+            nc.sync.dma_start(rows[:], xT[a * K_PASS : (a + 1) * K_PASS, :].rearrange("(o j) t -> o j t", j=PACK))
+            x_rows.append(rows)
             if a == 0:
-                slots = load_list("slots", offs)
+                slot_list = load_list("offs", offs)
             if a == 1:
                 nc.sync.dma_start(bias[:], b)
-        nc.sync.dma_start(gate_cols[:], gate[:, 0, :].rearrange("r (p i) -> p r i", p=P))
-        scale_rows = w_scales.rearrange("e a (quad q) n -> q quad (e a) n", q=4).bitcast(I32)
-        for q in range(4):
-            nc.sync.dma_start(w_planes[:].bitcast(I32)[q:P:32], scale_rows[q])
+        nc.sync.dma_start(gate_cols[:], gate[:, 0, :].rearrange("r (o i) -> o r i", o=P))
+        scale_rows = w_scales.rearrange("e a (quad q) n -> q quad (e a) n", q=QUAD_ROWS).bitcast(I32)
+        for q in range(QUAD_ROWS):
+            nc.sync.dma_start(w_planes[:].bitcast(I32)[q:P:QUAD], scale_rows[q])
         w_codes = {}
-        w_view = w_words.rearrange("e a p n r -> p (e a) (n r)").bitcast(I32)
-        for m0, m1 in runs(W_GROUPS):
-            words = keep.tile([P, m1 - m0, N], I32, name=f"w{m0}", align_bytes=64)
-            nc.sync.dma_start(words[:], w_view[:, m0:m1, :])
+        matrices = w_words.rearrange("e a o n r -> o (e a) (n r)").bitcast(I32)
+        for m0, m1 in runs(W_LOADS):
+            loaded = keep.tile([P, m1 - m0, N], I32, name=f"w{m0}", align_bytes=64)
+            nc.sync.dma_start(loaded[:], matrices[:, m0:m1, :])
             for m in range(m0, m1):
-                w_codes[divmod(m, PASSES)] = words[:, m - m0, :]
+                w_codes[divmod(m, PASSES)] = loaded[:, m - m0, :]
+            if m0 == 0:
+                pos_lists = [load_list(f"pos{r + 1}", src) for r, src in enumerate((pos1, pos2, pos3))]
 
-        lists = [load_list(f"pos{r + 1}", src) for r, src in enumerate((pos1, pos2, pos3))]
+        def gather_slots(dst, window, s0, s1):
+            nc.vector.tensor_copy(dst[:, s0:s1], window.indirect(slot_list[:, s0 // PER_COL : s1 // PER_COL]))
 
-        def gather(dst, window, s0, s1):
-            nc.vector.tensor_copy(dst[:, s0:s1], window.indirect(slots[:, s0 // PER_COL : s1 // PER_COL]))
-
-        slot_codes = []
-        all_codes = keep.tile([P, (PASSES + 1) * T], U32, align_bytes=64)
-        nc.vector.memset(all_codes[:, PASSES * T :], 0)
-        slot_planes = keep.tile([P, S], U8, align_bytes=64)
+        slot_words = []
+        token_words = keep.tile([P, (PASSES + 1) * T], U32, align_bytes=64)
+        nc.vector.memset(token_words[:, PASSES * T :], 0)
+        slot_plane = keep.tile([P, S], U8, align_bytes=64)
         for a in range(PASSES):
-            first = (PASSES - 1 - a) * T
-            codes = all_codes[:, first : first + T]
+            first = (LAST - a) * T
+            pass_words = token_words[:, first : first + T]
             for t0, t1 in runs(X_PIECES[a]):
-                raw = raws[a, t0]
-                grouped = keep.tile([P, t1 - t0, PACK], BF16, name=f"grouped{a}_{t0}", align_bytes=64)
-                dst = grouped[:].rearrange("p (c i) j -> p c j i", i=4)
-                src = raw.rearrange("p j (c i) -> p c j i", i=4)
-                if (a, t0) in VECTOR_TOKENS:
+                rounded = keep.tile([P, t1 - t0, PACK], BF16, name=f"rounded{a}_{t0}", align_bytes=64)
+                dst = rounded[:].rearrange("o (c i) j -> o c j i", i=LINE)
+                src = x_rows[a][:, :, t0:t1].rearrange("o j (c i) -> o c j i", i=LINE)
+                if (a, t0) in VECTOR_PIECES:
                     nc.vector.tensor_copy(dst, src)
                 else:
                     nc.scalar.activation(dst, src, COPY)
                 nc.vector.quantize_mx(
-                    codes[:, t0:t1].bitcast(FP8X4),
-                    x_planes[4 * a : P, t0:t1],
-                    grouped[:].rearrange("p w j -> p (w j)"),
+                    pass_words[:, t0:t1].bitcast(FP8X4),
+                    x_plane[QUAD_ROWS * a : P, t0:t1],
+                    rounded[:].rearrange("o t j -> o (t j)"),
                 )
-            picked = keep.tile([P, S], U32, name=f"picked{a}", align_bytes=64)
-            slot_codes.append(picked)
-            if a < PASSES - 1:
-                gather(picked, all_codes[:, first : first + 2 * T], 0, S)
+            picked = keep.tile([P, S], U32, name=f"slot_words{a}", align_bytes=64)
+            slot_words.append(picked)
+            if a < LAST:
+                gather_slots(picked, token_words[:, first : first + 2 * T], 0, S)
             else:
-                for s0, s1 in runs(LAST_WORD_CUTS):
-                    if s0 % HALF == 0:
-                        gather(slot_planes, x_planes[:], s0, s0 + HALF)
-                    gather(picked, codes, s0, s1)
+                for s0, s1 in runs(SLOT_GROUPS):
+                    if s0 % BYTE_SLOTS == 0:
+                        gather_slots(slot_plane, x_plane[:], s0, s0 + BYTE_SLOTS)
+                    gather_slots(picked, pass_words, s0, s1)
 
         gates = []
         for r in range(TOP):
             spread = keep.tile([P, T], F32, name=f"gate{r}")
-            for h in range(2):
-                bank = psum.tile([P, 4 * P], F32, name="bank")
-                for i in range(4):
-                    column = gate_cols[:, r, 4 * h + i : 4 * h + i + 1]
+            for h in range(T // P // BANK_BLOCKS):
+                bank = psum.tile([P, BANK_BLOCKS * P], F32, name="bank")
+                for i in range(BANK_BLOCKS):
+                    column = gate_cols[:, r, BANK_BLOCKS * h + i : BANK_BLOCKS * h + i + 1]
                     nc.tensor.transpose(bank[:, i * P : (i + 1) * P], column.to_broadcast([P, P]), ident[:])
                 nc.scalar.copy(
-                    spread[:].rearrange("n (p h i) -> n h p i", h=2, i=4)[:, h],
-                    bank[:].rearrange("n (i p) -> n p i", i=4),
+                    spread[:].rearrange("n (o h i) -> n h o i", o=P, i=BANK_BLOCKS)[:, h],
+                    bank[:].rearrange("n (i o) -> n o i", i=BANK_BLOCKS),
                 )
             gates.append(spread)
 
-        for e0, e1 in runs((E // 2,) + (1,) * (E // 2)):
-            group = range(e0, e1)
-            accs = {e: psum.tile([P, C], F32, name="bank") for e in group}
-            steps = [(e, a) for e in group for a in range(PASSES - 1)] + [(e, PASSES - 1) for e in group]
+        for s0, s1 in runs(SLOT_GROUPS):
+            experts = range(s0 // C, s1 // C)
+            sums = {e: psum.tile([P, C], F32, name="bank") for e in experts}
+            steps = [(e, a) for e in experts for a in range(LAST)] + [(e, LAST) for e in experts]
             for e, a in steps:
                 cols = slice(e * C, (e + 1) * C)
                 nc.tensor.matmul_mx(
-                    accs[e][:],
+                    sums[e][:],
                     lhsT=w_codes[e, a].bitcast(FP8X4),
                     lhsT_scale=w_planes[:, e * PASSES + a, :],
-                    rhs=slot_codes[a][:, cols].bitcast(FP8X4),
-                    rhs_scale=slot_planes[4 * a : P, cols],
+                    rhs=slot_words[a][:, cols].bitcast(FP8X4),
+                    rhs_scale=slot_plane[QUAD_ROWS * a : P, cols],
                     start=(a == 0),
-                    stop=(a == PASSES - 1),
+                    stop=(a == LAST),
                 )
-                if a == PASSES - 1:
-                    nc.scalar.activation(y[:, cols], accs[e][:], GELU, bias=bias[:, e : e + 1])
+                if a == LAST:
+                    nc.scalar.activation(y[:, cols], sums[e][:], GELU, bias=bias[:, e : e + 1])
 
-        chunks = runs(OUT_CUTS)
-        for t0, t1 in chunks:
+        for t0, t1 in runs(OUT_STRETCHES):
             width = t1 - t0
             blocks = runs((P,) * (width // P))
             on_tensor = t1 < T
@@ -173,11 +169,13 @@ def tile_moe_ecr_lin_gelu_kernel(
             turned = [psum.tile([P, P], F32, name="bank") for block in blocks] if on_tensor else []
             for r in range(TOP):
                 term = keep.tile([P, width], F32, name=f"term{r}_{t0}")
-                picks = lists[r][:, t0 // PER_COL : t1 // PER_COL]
+                picks = pos_lists[r][:, t0 // PER_COL : t1 // PER_COL]
                 nc.vector.tensor_tensor(term[:], y[:].indirect(picks), gates[r][:, t0:t1], MULT)
                 terms.append(term)
                 for bank, (c0, c1) in zip(turned, blocks):
-                    nc.tensor.matmul(bank[:], term[:, c0:c1], ident[:], start=(r == 0), stop=(r == TOP - 1), is_transpose=True)
+                    nc.tensor.matmul(
+                        bank[:], term[:, c0:c1], ident[:], start=(r == 0), stop=(r == TOP - 1), is_transpose=True
+                    )
             total = keep.tile([P, width], F32, name=f"total{t0}")
             if on_tensor:
                 by_token = keep.tile([P, width], F32, name=f"by_token{t0}")

from contextlib import ExitStack

import concourse.mybir as mybir
from concourse.masks import make_identity

K, T, E, C, N = 2048, 1024, 12, 128, 128
TOP = 3
PAD = 64
S = E * C
P = 128
PACK = 4
K_PASS = P * PACK
PASSES = K // K_PASS
LAST = PASSES - 1
PER_COL = 16
QUAD = 32
QUAD_ROWS = 4
LINE = 4
BANKS = 8
BANK_BLOCKS = 4

F32 = mybir.dt.float32
BF16 = mybir.dt.bfloat16
I32 = mybir.dt.int32
U32 = mybir.dt.uint32
U16 = mybir.dt.uint16
U8 = mybir.dt.uint8
FP8X4 = mybir.dt.float8_e4m3fn_x4
COPY = mybir.ActivationFunctionType.Copy
GELU = mybir.ActivationFunctionType.Gelu_apprx_tanh
MULT = mybir.AluOpType.mult
ADD = mybir.AluOpType.add

FLOPS = 2 * K * N * S
BYTES = 4 * K * T + E * K * N + E * K * N // 32 + 4 * N * E + 4 * TOP * T + 2 * P * (S + TOP * T) // PER_COL + 4 * N * T

X_PIECES = ((512, 256, 256), (512, 256, 256), (512, 256, 128, 128), (512, 256, 256))
VECTOR_PIECES = ((0, 0), (1, 768), (2, 896))
W_LOADS = (12, 12, 8, 8, 4, 3, 1)
SLOT_GROUPS = (768, 384, 256, 128)
BYTE_SLOTS = S // 2
OUT_STRETCHES = (512, 256, 256)


def runs(widths):
    ends = [sum(widths[: i + 1]) for i in range(len(widths))]
    return [(end - width, end) for width, end in zip(widths, ends)]


def tile_moe_ecr_lin_gelu_kernel(
    tc, xT, w_words, w_scales, b, gate, offs, pos1, pos2, pos3, out
):
    nc = tc.nc
    with ExitStack() as ctx:
        keep = ctx.enter_context(tc.tile_pool(name="keep", bufs=1))
        psum = ctx.enter_context(tc.psum_pool(name="psum", bufs=BANKS))

        def load_list(name, src):
            tile = keep.tile(list(src.shape), U16, name=name)
            nc.sync.dma_start(tile[:], src)
            return tile

        w_planes = keep.tile([P, E * PASSES, N], U8, align_bytes=64)
        nc.vector.memset(w_planes[:].bitcast(I32), 0)
        x_plane = keep.tile([P, T], U8, align_bytes=64)
        nc.vector.memset(x_plane[:].bitcast(I32), 0)
        zeros = keep.tile([P, PAD], F32)
        nc.vector.memset(zeros[:], 0.0)
        y = keep.tile([P, S + PAD], F32)
        nc.scalar.activation(y[:, S:], zeros[:], GELU)
        ident = keep.tile([P, P], F32)
        make_identity(nc, ident[:])

        gate_cols = keep.tile([P, TOP, T // P], F32)
        bias = keep.tile([P, E], F32)
        x_rows = []
        for a in range(PASSES):
            rows = keep.tile([P, PACK, T], F32, name=f"x_rows{a}")
            nc.sync.dma_start(rows[:], xT[a * K_PASS : (a + 1) * K_PASS, :].rearrange("(o j) t -> o j t", j=PACK))
            x_rows.append(rows)
            if a == 0:
                slot_list = load_list("offs", offs)
            if a == 1:
                nc.sync.dma_start(bias[:], b)
        nc.sync.dma_start(gate_cols[:], gate[:, 0, :].rearrange("r (o i) -> o r i", o=P))
        scale_rows = w_scales.rearrange("e a (quad q) n -> q quad (e a) n", q=QUAD_ROWS).bitcast(I32)
        for q in range(QUAD_ROWS):
            nc.sync.dma_start(w_planes[:].bitcast(I32)[q:P:QUAD], scale_rows[q])
        w_codes = {}
        matrices = w_words.rearrange("e a o n r -> o (e a) (n r)").bitcast(I32)
        for m0, m1 in runs(W_LOADS):
            loaded = keep.tile([P, m1 - m0, N], I32, name=f"w{m0}", align_bytes=64)
            nc.sync.dma_start(loaded[:], matrices[:, m0:m1, :])
            for m in range(m0, m1):
                w_codes[divmod(m, PASSES)] = loaded[:, m - m0, :]
            if m0 == 0:
                pos_lists = [load_list(f"pos{r + 1}", src) for r, src in enumerate((pos1, pos2, pos3))]

        def gather_slots(dst, window, s0, s1):
            nc.vector.tensor_copy(dst[:, s0:s1], window.indirect(slot_list[:, s0 // PER_COL : s1 // PER_COL]))

        slot_words = []
        token_words = keep.tile([P, (PASSES + 1) * T], U32, align_bytes=64)
        nc.vector.memset(token_words[:, PASSES * T :], 0)
        slot_plane = keep.tile([P, S], U8, align_bytes=64)
        for a in range(PASSES):
            first = (LAST - a) * T
            pass_words = token_words[:, first : first + T]
            for t0, t1 in runs(X_PIECES[a]):
                rounded = keep.tile([P, t1 - t0, PACK], BF16, name=f"rounded{a}_{t0}", align_bytes=64)
                dst = rounded[:].rearrange("o (c i) j -> o c j i", i=LINE)
                src = x_rows[a][:, :, t0:t1].rearrange("o j (c i) -> o c j i", i=LINE)
                if (a, t0) in VECTOR_PIECES:
                    nc.vector.tensor_copy(dst, src)
                else:
                    nc.scalar.activation(dst, src, COPY)
                nc.vector.quantize_mx(
                    pass_words[:, t0:t1].bitcast(FP8X4),
                    x_plane[QUAD_ROWS * a : P, t0:t1],
                    rounded[:].rearrange("o t j -> o (t j)"),
                )
            picked = keep.tile([P, S], U32, name=f"slot_words{a}", align_bytes=64)
            slot_words.append(picked)
            if a < LAST:
                gather_slots(picked, token_words[:, first : first + 2 * T], 0, S)
            else:
                for s0, s1 in runs(SLOT_GROUPS):
                    if s0 % BYTE_SLOTS == 0:
                        gather_slots(slot_plane, x_plane[:], s0, s0 + BYTE_SLOTS)
                    gather_slots(picked, pass_words, s0, s1)

        gates = []
        for r in range(TOP):
            spread = keep.tile([P, T], F32, name=f"gate{r}")
            for h in range(T // P // BANK_BLOCKS):
                bank = psum.tile([P, BANK_BLOCKS * P], F32, name="bank")
                for i in range(BANK_BLOCKS):
                    column = gate_cols[:, r, BANK_BLOCKS * h + i : BANK_BLOCKS * h + i + 1]
                    nc.tensor.transpose(bank[:, i * P : (i + 1) * P], column.to_broadcast([P, P]), ident[:])
                nc.scalar.copy(
                    spread[:].rearrange("n (o h i) -> n h o i", o=P, i=BANK_BLOCKS)[:, h],
                    bank[:].rearrange("n (i o) -> n o i", i=BANK_BLOCKS),
                )
            gates.append(spread)

        for s0, s1 in runs(SLOT_GROUPS):
            experts = range(s0 // C, s1 // C)
            sums = {e: psum.tile([P, C], F32, name="bank") for e in experts}
            steps = [(e, a) for e in experts for a in range(LAST)] + [(e, LAST) for e in experts]
            for e, a in steps:
                cols = slice(e * C, (e + 1) * C)
                nc.tensor.matmul_mx(
                    sums[e][:],
                    lhsT=w_codes[e, a].bitcast(FP8X4),
                    lhsT_scale=w_planes[:, e * PASSES + a, :],
                    rhs=slot_words[a][:, cols].bitcast(FP8X4),
                    rhs_scale=slot_plane[QUAD_ROWS * a : P, cols],
                    start=(a == 0),
                    stop=(a == LAST),
                )
                if a == LAST:
                    nc.scalar.activation(y[:, cols], sums[e][:], GELU, bias=bias[:, e : e + 1])

        for t0, t1 in runs(OUT_STRETCHES):
            width = t1 - t0
            blocks = runs((P,) * (width // P))
            on_tensor = t1 < T
            terms = []
            turned = [psum.tile([P, P], F32, name="bank") for block in blocks] if on_tensor else []
            for r in range(TOP):
                term = keep.tile([P, width], F32, name=f"term{r}_{t0}")
                picks = pos_lists[r][:, t0 // PER_COL : t1 // PER_COL]
                nc.vector.tensor_tensor(term[:], y[:].indirect(picks), gates[r][:, t0:t1], MULT)
                terms.append(term)
                for bank, (c0, c1) in zip(turned, blocks):
                    nc.tensor.matmul(
                        bank[:], term[:, c0:c1], ident[:], start=(r == 0), stop=(r == TOP - 1), is_transpose=True
                    )
            total = keep.tile([P, width], F32, name=f"total{t0}")
            if on_tensor:
                by_token = keep.tile([P, width], F32, name=f"by_token{t0}")
                back = psum.tile([P, width], F32, name="bank")
                for bank, (c0, c1) in zip(turned, blocks):
                    nc.scalar.copy(by_token[:, c0:c1], bank[:])
                    nc.tensor.transpose(back[:, c0:c1], by_token[:, c0:c1], ident[:])
                nc.scalar.copy(total[:], back[:])
            else:
                pair = keep.tile([P, width], F32)
                nc.vector.tensor_tensor(pair[:], terms[0][:], terms[1][:], ADD)
                nc.vector.tensor_tensor(total[:], pair[:], terms[2][:], ADD)
            nc.sync.dma_start(out[:, t0:t1], total[:])
